import numpy as np
import ml_dtypes


def mxq(x, axis, fmt="e4m3"):
    dtype, down = {"e4m3": (ml_dtypes.float8_e4m3fn, 7), "e5m2": (ml_dtypes.float8_e5m2, 14)}[fmt]
    v = np.moveaxis(np.asarray(x, np.float32).astype(ml_dtypes.bfloat16).astype(np.float64), axis, -1)
    blocks = v.reshape(v.shape[:-1] + (-1, 32))
    amax = np.abs(blocks).max(-1, keepdims=True)
    byte = np.maximum(np.where(amax > 0, np.frexp(amax)[1] - 1 + 127, 0) - down, 1)
    scale = np.exp2(byte - 127.0)
    codes = (blocks / scale).astype(np.float32).astype(dtype).astype(np.float64)
    return np.moveaxis((codes * scale).reshape(v.shape), -1, axis)


WIDE = False


def mx_kscale(k):
    if not WIDE:
        return np.ones(k)
    levels = np.array([18, -18])
    if k % 512:
        return np.exp2(np.random.permutation(np.resize(levels, k // 32))).repeat(32)
    a = np.empty((k // 512, 16))
    for p in range(k // 512):
        a[p, :8] = np.random.permutation(np.resize(levels, 8))
        for g in range(8):
            far = levels[np.abs(levels - a[p, g]) >= 10]
            a[p, g + 8] = far[np.random.randint(len(far))]
    return np.exp2(a.ravel()).repeat(32)


def f64(x):
    return np.asarray(x).astype(np.float64)


def striped(idx):
    return np.tile(np.asarray(idx).reshape(-1, 16).T, (8, 1)).astype(np.uint16)


def unstriped(offs):
    return offs[:16].T.reshape(-1).astype(np.int64)


E2M1 = np.array([0.0, 0.5, 1.0, 1.5, 2.0, 3.0, 4.0, 6.0, -0.0, -0.5, -1.0, -1.5, -2.0, -3.0, -4.0, -6.0])


def pack_weight(w, fmt):
    k, n = w.shape
    w = f64(np.asarray(w, np.float32).astype(ml_dtypes.bfloat16)).reshape(k // 32, 32, n)
    amax = np.abs(w).max(1)
    if fmt == "e4m3":
        byte = np.frexp(amax)[1] - 1 + 127 - 7
    else:
        mant, ex = np.frexp(amax / 6.0)
        byte = np.where(mant > 0.5, ex, ex - 1) + 127
    byte = np.clip(np.where(amax > 0, byte, 1), 1, 254)
    scaled = (w * np.exp2(127.0 - byte)[:, None, :]).reshape(k, n).astype(np.float32)
    by_word = np.ascontiguousarray(scaled.reshape(k // 512, 128, 4, n).transpose(0, 1, 3, 2))
    if fmt == "e4m3":
        words = by_word.astype(ml_dtypes.float8_e4m3fn).view(np.uint8)
    else:
        c = by_word.astype(ml_dtypes.float4_e2m1fn).view(np.uint8) & 0xF
        words = (c[..., 0::2] | (c[..., 1::2] << 4)).reshape(k // 512, 128, 2 * n)
    return np.ascontiguousarray(words), np.ascontiguousarray(byte.astype(np.uint8).reshape(k // 512, 16, n))


def unpack_weight(words, scales, fmt):
    g, _, n = scales.shape
    words = np.ascontiguousarray(words).reshape(g, 128, n, -1)
    if fmt == "e4m3":
        vals = words.view(ml_dtypes.float8_e4m3fn).astype(np.float64)
    else:
        nib = np.empty((g, 128, n, 4), np.uint8)
        nib[..., 0::2] = words & 0xF
        nib[..., 1::2] = words >> 4
        vals = E2M1[nib]
    vals = vals * np.repeat(np.exp2(scales.astype(np.float64) - 127.0), 8, axis=1)[..., None]
    return vals.transpose(0, 1, 3, 2).reshape(g * 512, n)


def setup_inputs():
    n = np.random.standard_normal
    uni = np.random.uniform
    nbr = np.random.randint(0, 1024, 2048)
    f_f = mx_kscale(512)
    f_m = mx_kscale(512)
    w1_ = pack_weight(n((512, 512)) / np.sqrt(512) / f_f[:, None], "e2m1")
    return {
        "dyT": (n((512, 1024)) * f_m[:, None]).astype(np.float32),
        "w2": (n((512, 512)) / np.sqrt(512) / f_m[:, None] * f_f[None, :]).astype(np.float32),
        "w1_words": w1_[0],
        "w1_scales": w1_[1],
        "hT": (np.tanh(2.0 * n((512, 1024)))).astype(np.float32),
        "offs": striped(nbr),
    }


def reference(dyT, w2, w1_words, w1_scales, hT, offs):
    nbr = unstriped(offs)
    w1 = unpack_weight(w1_words, w1_scales, "e2m1")
    u = mxq(f64(w2), 0, "e4m3").T @ mxq(f64(dyT), 0, "e5m2")
    u_c = u[:, nbr]
    su = u_c.reshape(512, 1024, 2).sum(-1)
    dh = su * (1.0 - np.square(f64(hT)))
    w = w1.T @ mxq(dh, 0, "e5m2")
    w_c = w[:, nbr]
    out = w_c.reshape(512, 1024, 2).sum(-1)
    return out

@@ -1,0 +1,217 @@
+from contextlib import ExitStack
+
+import concourse.mybir as mybir
+from concourse.masks import make_identity
+
+F32 = mybir.dt.float32
+BF16 = mybir.dt.bfloat16
+I32 = mybir.dt.int32
+U32 = mybir.dt.uint32
+U16 = mybir.dt.uint16
+U8 = mybir.dt.uint8
+E4M3 = mybir.dt.float8_e4m3fn_x4
+E5M2 = mybir.dt.float8_e5m2_x4
+E2M1 = mybir.dt.float4_e2m1fn_x4
+ACT = mybir.ActivationFunctionType
+ALU = mybir.AluOpType
+
+P = 128
+PACK = 4
+FEAT = 512
+NODES = 1024
+DEG = 2
+PLANES = FEAT // P
+BLOCKS = NODES // P
+BANK = 512
+HALVES = NODES // BANK
+DY_CHUNK = 256
+VEC_SHARE = 160
+FLOPS = 2 * 2 * FEAT * FEAT * NODES
+
+
+def tile_attend_ggcn2_tnh_kernel(tc, dyT, w2, w1_words, w1_scales, hT, offs, out):
+    nc = tc.nc
+    with ExitStack() as ctx:
+        keep = ctx.enter_context(tc.tile_pool(name="keep", bufs=1))
+        ring = ctx.enter_context(tc.tile_pool(name="ring", bufs=2))
+        psum = ctx.enter_context(tc.psum_pool(name="psum", bufs=2))
+
+        offsets = keep.tile([P, NODES * DEG // 16], U16, name="offsets")
+        ident = keep.tile([P, P], F32, name="ident")
+        w1_sc = keep.tile([P, FEAT], U8, name="w1_sc", align_bytes=64)
+        w1_cd = keep.tile([P, 2 * FEAT], U8, name="w1_cd", align_bytes=64)
+
+        w2_rows = w2.rearrange("(p j) f -> p j f", j=PACK)
+        dy_rows = dyT.rearrange("(p j) x -> p j x", j=PACK)
+        h_rows = hT.rearrange("(a p) x -> p a x", p=P)
+
+        def load(name, src, width):
+            t = keep.tile([P, PACK, width], F32, name=name)
+            nc.sync.dma_start(out=t[:], in_=src)
+            return t
+
+        w2_first = load("w2_first", w2_rows[:, :, 0:P], P)
+        dy_raw = [load(f"dy_raw{c}", dy_rows[:, :, c * DY_CHUNK:(c + 1) * DY_CHUNK], DY_CHUNK)
+                  for c in range(NODES // DY_CHUNK)]
+        w2_second = load("w2_second", w2_rows[:, :, P:2 * P], P)
+        nc.sync.dma_start(offsets[:], offs)
+        w2_rest = load("w2_rest", w2_rows[:, :, 2 * P:FEAT], 2 * P)
+        h_raw = [load(f"h_raw{c}", h_rows[:, :, c * 2 * P:(c + 1) * 2 * P], 2 * P) for c in range(BLOCKS // 2)]
+        w2_raw = [w2_first[:], w2_second[:], w2_rest[:, :, 0:P], w2_rest[:, :, P:2 * P]]
+
+        make_identity(nc, ident[:])
+        nc.gpsimd.memset(w1_sc[:].bitcast(U32), 0)
+        nc.sync.dma_start(out=w1_cd[:].bitcast(I32), in_=w1_words[0].bitcast(I32))
+        for q in range(4):
+            nc.sync.dma_start(out=w1_sc[32 * q:32 * q + 4, :].bitcast(I32),
+                              in_=w1_scales[0, 4 * q:4 * q + 4, :].bitcast(I32))
+
+        def interleave(copy, dst, src):
+            copy(out=dst.rearrange("p (c i) t -> p c t i", i=4), in_=src.rearrange("p t (c i) -> p c t i", i=4))
+
+        w2_cd = [keep.tile([P, P], U32, name=f"w2_cd{a}", align_bytes=64) for a in range(PLANES)]
+        w2_sc = [keep.tile([P, P], U8, name=f"w2_sc{a}", align_bytes=64) for a in range(PLANES)]
+
+        def quantise_w2(a, copy):
+            grouped = keep.tile([P, P, PACK], BF16, name=f"w2_bf{a}", align_bytes=64)
+            interleave(copy, grouped[:], w2_raw[a])
+            nc.vector.quantize_mx(out=w2_cd[a][:].bitcast(E4M3), scales=w2_sc[a][:],
+                                  in_=grouped[:].rearrange("p c t -> p (c t)"))
+
+        dy_cd = keep.tile([P, NODES], U32, name="dy_cd", align_bytes=64)
+        dy_sc = keep.tile([P, NODES], U8, name="dy_sc", align_bytes=64)
+
+        def quantise_dy(c):
+            grouped = keep.tile([P, DY_CHUNK, PACK], BF16, name=f"dy_bf{c}", align_bytes=64)
+            interleave(nc.scalar.copy, grouped[:, VEC_SHARE:, :], dy_raw[c][:, :, VEC_SHARE:])
+            interleave(nc.vector.tensor_copy, grouped[:, :VEC_SHARE, :], dy_raw[c][:, :, :VEC_SHARE])
+            cols = slice(c * DY_CHUNK, (c + 1) * DY_CHUNK)
+            nc.vector.quantize_mx(out=dy_cd[:, cols].bitcast(E5M2), scales=dy_sc[:, cols],
+                                  in_=grouped[:].rearrange("p c t -> p (c t)"))
+
+        u_win = [keep.tile([P, NODES], F32, name=f"u_win{a}") for a in range(PLANES)]
+        w_win = [keep.tile([P, NODES], F32, name=f"w_win{a}") for a in range(PLANES)]
+
+        def upper(a, half, copy):
+            cols = slice(half * BANK, (half + 1) * BANK)
+            acc = psum.tile([P, BANK], F32, name="acc", tag="mm")
+            nc.tensor.matmul_mx(out=acc[:], lhsT=w2_cd[a][:].bitcast(E4M3), lhsT_scale=w2_sc[a][:],
+                                rhs=dy_cd[:, cols].bitcast(E5M2), rhs_scale=dy_sc[:, cols], start=True, stop=True)
+            copy(out=u_win[a][:, cols], in_=acc[:])
+
+        def gather(window, first, count):
+            picked = ring.tile([P, DEG, count * P], F32, name="picked", tag="picked", bufs=6)
+            nc.vector.tensor_copy(
+                out=picked[:].bitcast(U32).rearrange("p j x -> p x j"),
+                in_=window[:].bitcast(U32).indirect(offsets[:, 16 * first:16 * (first + count)]))
+            return picked
+
+        def sum_turned(dst, picked, k):
+            for j in range(DEG):
+                nc.tensor.matmul(dst, picked[:, j, k * P:(k + 1) * P], ident[:], is_transpose=True,
+                                 start=(j == 0), stop=(j == DEG - 1))
+
+        h_sq = [keep.tile([P, FEAT], F32, name=f"h_sq{b}") for b in range(BLOCKS)]
+
+        def square_h(b):
+            turned = psum.tile([P, PLANES, P], F32, name="turned", tag="turn")
+            for a in range(PLANES):
+                nc.tensor.transpose(turned[:, a, :], h_raw[b // 2][:, a, (b % 2) * P:(b % 2 + 1) * P], ident[:])
+            nc.scalar.activation(out=h_sq[b][:], in_=turned[:].rearrange("p a f -> p (a f)"), func=ACT.Square)
+
+        dh_cd = keep.tile([P, NODES], U32, name="dh_cd", align_bytes=64)
+        dh_sc = keep.tile([P, NODES], U8, name="dh_sc", align_bytes=64)
+        su = {}
+        dh_bf = {}
+
+        def sum_upper(a, first, count):
+            picked = gather(u_win[a], first, count)
+            for k in range(count):
+                if a == 0:
+                    su[first + k] = psum.tile([P, PLANES, P], F32, name="su", tag="sum", bufs=4)
+                sum_turned(su[first + k][:, a, :], picked, k)
+
+        def through_tanh(b):
+            neg = keep.tile([P, FEAT], BF16, name=f"neg_dh{b}")
+            nc.vector.scalar_tensor_tensor(out=neg[:], in0=h_sq[b][:], scalar=1.0,
+                                           in1=su[b][:].rearrange("p a f -> p (a f)"),
+                                           op0=ALU.subtract, op1=ALU.mult)
+            words = neg[:].bitcast(F32)
+            back = psum.tile([P, 2, P], F32, name="back", tag="turn")
+            for s in range(2):
+                nc.tensor.transpose(back[:, s, :], words[:, s::2], ident[:])
+            dh_bf[b] = keep.tile([P, P * PACK], BF16, name=f"dh_bf{b}", align_bytes=64)
+            nc.scalar.copy(out=dh_bf[b][:].bitcast(F32).rearrange("p (x s) -> p x s", s=2),
+                           in_=back[:].rearrange("p s x -> p x s"))
+
+        def quantise_dh(b):
+            cols = slice(b * P, (b + 1) * P)
+            nc.vector.quantize_mx(out=dh_cd[:, cols].bitcast(E5M2), scales=dh_sc[:, cols], in_=dh_bf[b][:])
+
+        def lower(a, half, on_vector):
+            cols = slice(half * BANK, (half + 1) * BANK)
+            acc = psum.tile([P, BANK], F32, name="acc", tag="mm")
+            nc.tensor.matmul_mx(out=acc[:], lhsT=w1_cd[:, 2 * a * P:2 * (a + 1) * P].bitcast(E2M1),
+                                lhsT_scale=w1_sc[:, a * P:(a + 1) * P],
+                                rhs=dh_cd[:, cols].bitcast(E5M2), rhs_scale=dh_sc[:, cols], start=True, stop=True)
+            if on_vector:
+                nc.vector.tensor_scalar_mul(w_win[a][:, cols], acc[:], -1.0)
+            else:
+                nc.scalar.activation(out=w_win[a][:, cols], in_=acc[:], func=ACT.Copy, scale=-1.0)
+
+        quantise_w2(0, nc.vector.tensor_copy)
+        quantise_dy(0)
+        quantise_dy(1)
+        upper(0, 0, nc.scalar.copy)
+        quantise_dy(2)
+        quantise_dy(3)
+        upper(0, 1, nc.vector.tensor_copy)
+
+        for a in range(PLANES):
+            if a + 1 < PLANES:
+                quantise_w2(a + 1, nc.scalar.copy)
+                for half in range(HALVES):
+                    upper(a + 1, half, nc.scalar.copy)
+            sum_upper(a, 0, 2)
+            sum_upper(a, 2, 2)
+        for b in range(BLOCKS):
+            square_h(b)
+        for first in (4, 6):
+            through_tanh(first - 4)
+            through_tanh(first - 3)
+            for a in range(PLANES):
+                sum_upper(a, first, 2)
+            quantise_dh(first - 4)
+            quantise_dh(first - 3)
+        for a in range(PLANES):
+            lower(a, 0, False)
+        for b in range(4, BLOCKS):
+            through_tanh(b)
+        for b in range(4, BLOCKS):
+            quantise_dh(b)
+        for a in range(PLANES):
+            lower(a, 1, a == 0)
+
+        for a in range(PLANES):
+            for half in range(HALVES):
+                rows = slice(a * P, (a + 1) * P)
+                if (a, half) == (PLANES - 1, HALVES - 1):
+                    for first in (4, 6):
+                        picked = gather(w_win[a], first, 2)
+                        res = ring.tile([P, 2 * P], F32, name="res_tail")
+                        nc.vector.tensor_tensor(out=res[:], in0=picked[:, 0, :], in1=picked[:, 1, :], op=ALU.add)
+                        nc.sync.dma_start(out=out[rows, first * P:(first + 2) * P], in_=res[:])
+                    continue
+                so = psum.tile([P, 4, P], F32, name="so", tag="sum", bufs=4)
+                for piece in range(2):
+                    picked = gather(w_win[a], 4 * half + 2 * piece, 2)
+                    for k in range(2):
+                        sum_turned(so[:, 2 * piece + k, :], picked, k)
+                so_sb = ring.tile([P, 4, P], F32, name="so_sb")
+                nc.scalar.copy(out=so_sb[:], in_=so[:])
+                upright = psum.tile([P, 4, P], F32, name="upright", tag="turn")
+                for k in range(4):
+                    nc.tensor.transpose(upright[:, k, :], so_sb[:, k, :], ident[:])
+                res = ring.tile([P, BANK], F32, name="res", bufs=3)
+                nc.scalar.copy(out=res[:], in_=upright[:].rearrange("p k x -> p (k x)"))
+                nc.sync.dma_start(out=out[rows, half * BANK:(half + 1) * BANK], in_=res[:])

@@ -24,8 +24,8 @@ PLANES = FEAT // P
 BLOCKS = NODES // P
 BANK = 512
 HALVES = NODES // BANK
-DY_CHUNK = 256
-VEC_SHARE = 160
+DY_CHUNKS = ((0, 256), (256, 256), (512, 256), (768, 256))
+WINDOW = 1376
 FLOPS = 2 * 2 * FEAT * FEAT * NODES
 
 
@@ -51,14 +51,20 @@ def tile_attend_ggcn2_tnh_kernel(tc, dyT, w2, w1_words, w1_scales, hT, offs, out
             return t
 
         w2_first = load("w2_first", w2_rows[:, :, 0:P], P)
-        dy_raw = [load(f"dy_raw{c}", dy_rows[:, :, c * DY_CHUNK:(c + 1) * DY_CHUNK], DY_CHUNK)
-                  for c in range(NODES // DY_CHUNK)]
+        dy_raw = [load(f"dy_raw{x0}", dy_rows[:, :, x0:x0 + n], n) for x0, n in DY_CHUNKS]
         w2_second = load("w2_second", w2_rows[:, :, P:2 * P], P)
         nc.sync.dma_start(offsets[:], offs)
         w2_rest = load("w2_rest", w2_rows[:, :, 2 * P:FEAT], 2 * P)
         h_raw = [load(f"h_raw{c}", h_rows[:, :, c * 2 * P:(c + 1) * 2 * P], 2 * P) for c in range(BLOCKS // 2)]
         w2_raw = [w2_first[:], w2_second[:], w2_rest[:, :, 0:P], w2_rest[:, :, P:2 * P]]
 
+        u_all = keep.tile([P, (PLANES - 1) * NODES + WINDOW], F32, name="u_all", tag="u_all")
+        w_all = keep.tile([P, (PLANES - 1) * NODES + WINDOW], F32, name="w_all")
+        for table in (u_all, w_all):
+            nc.vector.memset(table[:, PLANES * NODES:], 0.0)
+        starts = [(PLANES - 1 - a) * NODES for a in range(PLANES)]
+        u_win = [u_all[:, s:s + WINDOW] for s in starts]
+        w_win = [w_all[:, s:s + WINDOW] for s in starts]
         make_identity(nc, ident[:])
         nc.gpsimd.memset(w1_sc[:].bitcast(U32), 0)
         nc.sync.dma_start(out=w1_cd[:].bitcast(I32), in_=w1_words[0].bitcast(I32))
@@ -82,15 +88,15 @@ def tile_attend_ggcn2_tnh_kernel(tc, dyT, w2, w1_words, w1_scales, hT, offs, out
         dy_sc = keep.tile([P, NODES], U8, name="dy_sc", align_bytes=64)
 
         def quantise_dy(c):
-            grouped = keep.tile([P, DY_CHUNK, PACK], BF16, name=f"dy_bf{c}", align_bytes=64)
-            interleave(nc.scalar.copy, grouped[:, VEC_SHARE:, :], dy_raw[c][:, :, VEC_SHARE:])
-            interleave(nc.vector.tensor_copy, grouped[:, :VEC_SHARE, :], dy_raw[c][:, :, :VEC_SHARE])
-            cols = slice(c * DY_CHUNK, (c + 1) * DY_CHUNK)
+            x0, n = DY_CHUNKS[c]
+            cut = 9 * n // 16
+            grouped = keep.tile([P, n, PACK], BF16, name=f"dy_bf{c}", align_bytes=64)
+            interleave(nc.scalar.copy, grouped[:, cut:, :], dy_raw[c][:, :, cut:])
+            interleave(nc.vector.tensor_copy, grouped[:, :cut, :], dy_raw[c][:, :, :cut])
+            cols = slice(x0, x0 + n)
             nc.vector.quantize_mx(out=dy_cd[:, cols].bitcast(E5M2), scales=dy_sc[:, cols],
                                   in_=grouped[:].rearrange("p c t -> p (c t)"))
 
-        u_win = [keep.tile([P, NODES], F32, name=f"u_win{a}") for a in range(PLANES)]
-        w_win = [keep.tile([P, NODES], F32, name=f"w_win{a}") for a in range(PLANES)]
 
         def upper(a, half, copy):
             cols = slice(half * BANK, (half + 1) * BANK)
@@ -100,10 +106,10 @@ def tile_attend_ggcn2_tnh_kernel(tc, dyT, w2, w1_words, w1_scales, hT, offs, out
             copy(out=u_win[a][:, cols], in_=acc[:])
 
         def gather(window, first, count):
-            picked = ring.tile([P, DEG, count * P], F32, name="picked", tag="picked", bufs=6)
+            picked = ring.tile([P, DEG, count * P], F32, name="picked", tag="picked", bufs=3)
             nc.vector.tensor_copy(
                 out=picked[:].bitcast(U32).rearrange("p j x -> p x j"),
-                in_=window[:].bitcast(U32).indirect(offsets[:, 16 * first:16 * (first + count)]))
+                in_=window.bitcast(U32).indirect(offsets[:, 16 * first:16 * (first + count)]))
             return picked
 
         def sum_turned(dst, picked, k):
@@ -111,7 +117,7 @@ def tile_attend_ggcn2_tnh_kernel(tc, dyT, w2, w1_words, w1_scales, hT, offs, out
                 nc.tensor.matmul(dst, picked[:, j, k * P:(k + 1) * P], ident[:], is_transpose=True,
                                  start=(j == 0), stop=(j == DEG - 1))
 
-        h_sq = [keep.tile([P, FEAT], F32, name=f"h_sq{b}") for b in range(BLOCKS)]
+        h_sq = [keep.tile([P, FEAT], F32, name=f"h_sq{b}", tag=f"h_sq{b}", align_bytes=64) for b in range(BLOCKS)]
 
         def square_h(b):
             turned = psum.tile([P, PLANES, P], F32, name="turned", tag="turn")
@@ -119,10 +125,11 @@ def tile_attend_ggcn2_tnh_kernel(tc, dyT, w2, w1_words, w1_scales, hT, offs, out
                 nc.tensor.transpose(turned[:, a, :], h_raw[b // 2][:, a, (b % 2) * P:(b % 2 + 1) * P], ident[:])
             nc.scalar.activation(out=h_sq[b][:], in_=turned[:].rearrange("p a f -> p (a f)"), func=ACT.Square)
 
-        dh_cd = keep.tile([P, NODES], U32, name="dh_cd", align_bytes=64)
-        dh_sc = keep.tile([P, NODES], U8, name="dh_sc", align_bytes=64)
+        dh_cd = {}
+        dh_sc = [keep.tile([P, BANK], U8, name=f"dh_sc{half}", align_bytes=64) for half in range(HALVES)]
         su = {}
-        dh_bf = {}
+        groups = ((0, 4), (4, 2), (6, 1), (7, 1))
+        dh_bf = [keep.tile([P, count * P * PACK], BF16, name=f"dh_bf{first}", align_bytes=64) for first, count in groups]
 
         def sum_upper(a, first, count):
             picked = gather(u_win[a], first, count)
@@ -132,7 +139,7 @@ def tile_attend_ggcn2_tnh_kernel(tc, dyT, w2, w1_words, w1_scales, hT, offs, out
                 sum_turned(su[first + k][:, a, :], picked, k)
 
         def through_tanh(b):
-            neg = keep.tile([P, FEAT], BF16, name=f"neg_dh{b}")
+            neg = keep.tile([P, FEAT], BF16, name=f"neg_dh{b}", tag="u_all" if b == 6 else f"neg_dh{b}")
             nc.vector.scalar_tensor_tensor(out=neg[:], in0=h_sq[b][:], scalar=1.0,
                                            in1=su[b][:].rearrange("p a f -> p (a f)"),
                                            op0=ALU.subtract, op1=ALU.mult)
@@ -140,20 +147,26 @@ def tile_attend_ggcn2_tnh_kernel(tc, dyT, w2, w1_words, w1_scales, hT, offs, out
             back = psum.tile([P, 2, P], F32, name="back", tag="turn")
             for s in range(2):
                 nc.tensor.transpose(back[:, s, :], words[:, s::2], ident[:])
-            dh_bf[b] = keep.tile([P, P * PACK], BF16, name=f"dh_bf{b}", align_bytes=64)
-            nc.scalar.copy(out=dh_bf[b][:].bitcast(F32).rearrange("p (x s) -> p x s", s=2),
+            g = max(i for i, (first, count) in enumerate(groups) if first <= b)
+            k = b - groups[g][0]
+            nc.scalar.copy(out=dh_bf[g][:].bitcast(F32)[:, 2 * P * k:2 * P * (k + 1)].rearrange("p (x s) -> p x s", s=2),
                            in_=back[:].rearrange("p s x -> p x s"))
 
-        def quantise_dh(b):
-            cols = slice(b * P, (b + 1) * P)
-            nc.vector.quantize_mx(out=dh_cd[:, cols].bitcast(E5M2), scales=dh_sc[:, cols], in_=dh_bf[b][:])
+        def quantise_dh(g):
+            first, count = groups[g]
+            half, k = divmod(first, 4)
+            if k == 0:
+                dh_cd[half] = keep.tile([P, BANK], U32, name=f"dh_cd{half}", align_bytes=64,
+                                        tag="h_sq7" if half == 0 else "dh_cd1")
+            cols = slice(k * P, (k + count) * P)
+            nc.vector.quantize_mx(out=dh_cd[half][:, cols].bitcast(E5M2), scales=dh_sc[half][:, cols], in_=dh_bf[g][:])
 
         def lower(a, half, on_vector):
             cols = slice(half * BANK, (half + 1) * BANK)
             acc = psum.tile([P, BANK], F32, name="acc", tag="mm")
             nc.tensor.matmul_mx(out=acc[:], lhsT=w1_cd[:, 2 * a * P:2 * (a + 1) * P].bitcast(E2M1),
                                 lhsT_scale=w1_sc[:, a * P:(a + 1) * P],
-                                rhs=dh_cd[:, cols].bitcast(E5M2), rhs_scale=dh_sc[:, cols], start=True, stop=True)
+                                rhs=dh_cd[half][:].bitcast(E5M2), rhs_scale=dh_sc[half][:], start=True, stop=True)
             if on_vector:
                 nc.vector.tensor_scalar_mul(w_win[a][:, cols], acc[:], -1.0)
             else:
@@ -172,46 +185,54 @@ def tile_attend_ggcn2_tnh_kernel(tc, dyT, w2, w1_words, w1_scales, hT, offs, out
                 quantise_w2(a + 1, nc.scalar.copy)
                 for half in range(HALVES):
                     upper(a + 1, half, nc.scalar.copy)
-            sum_upper(a, 0, 2)
-            sum_upper(a, 2, 2)
+            sum_upper(a, 0, 4)
         for b in range(BLOCKS):
             square_h(b)
-        for first in (4, 6):
-            through_tanh(first - 4)
-            through_tanh(first - 3)
-            for a in range(PLANES):
-                sum_upper(a, first, 2)
-            quantise_dh(first - 4)
-            quantise_dh(first - 3)
+        for b in range(4):
+            through_tanh(b)
         for a in range(PLANES):
-            lower(a, 0, False)
+            sum_upper(a, 4, 3)
+        for a in range(PLANES):
+            sum_upper(a, 7, 1)
         for b in range(4, BLOCKS):
             through_tanh(b)
-        for b in range(4, BLOCKS):
-            quantise_dh(b)
-        for a in range(PLANES):
-            lower(a, 1, a == 0)
-
-        for a in range(PLANES):
+        quantise_dh(0)
+        lower(0, 0, False)
+        for g in range(1, len(groups)):
+            quantise_dh(g)
+        lower(0, 1, True)
+        for a in range(1, PLANES):
             for half in range(HALVES):
-                rows = slice(a * P, (a + 1) * P)
-                if (a, half) == (PLANES - 1, HALVES - 1):
-                    for first in (4, 6):
-                        picked = gather(w_win[a], first, 2)
-                        res = ring.tile([P, 2 * P], F32, name="res_tail")
-                        nc.vector.tensor_tensor(out=res[:], in0=picked[:, 0, :], in1=picked[:, 1, :], op=ALU.add)
-                        nc.sync.dma_start(out=out[rows, first * P:(first + 2) * P], in_=res[:])
-                    continue
-                so = psum.tile([P, 4, P], F32, name="so", tag="sum", bufs=4)
-                for piece in range(2):
-                    picked = gather(w_win[a], 4 * half + 2 * piece, 2)
-                    for k in range(2):
-                        sum_turned(so[:, 2 * piece + k, :], picked, k)
-                so_sb = ring.tile([P, 4, P], F32, name="so_sb")
-                nc.scalar.copy(out=so_sb[:], in_=so[:])
-                upright = psum.tile([P, 4, P], F32, name="upright", tag="turn")
-                for k in range(4):
-                    nc.tensor.transpose(upright[:, k, :], so_sb[:, k, :], ident[:])
-                res = ring.tile([P, BANK], F32, name="res", bufs=3)
-                nc.scalar.copy(out=res[:], in_=upright[:].rearrange("p k x -> p (k x)"))
-                nc.sync.dma_start(out=out[rows, half * BANK:(half + 1) * BANK], in_=res[:])
+                lower(a, half, False)
+
+        def sum_on_tensor(a, first, count):
+            so = psum.tile([P, count, P], F32, name="so", tag="sum", bufs=4)
+            picked = gather(w_win[a], first, count)
+            for k in range(count):
+                sum_turned(so[:, k, :], picked, k)
+            so_sb = ring.tile([P, count, P], F32, name="so_sb")
+            nc.scalar.copy(out=so_sb[:], in_=so[:])
+            upright = psum.tile([P, count, P], F32, name="upright", tag="turn")
+            for k in range(count):
+                nc.tensor.transpose(upright[:, k, :], so_sb[:, k, :], ident[:])
+            res = ring.tile([P, count * P], F32, name="res", bufs=4)
+            nc.scalar.copy(out=res[:], in_=upright[:].rearrange("p k x -> p (k x)"))
+            nc.scalar.dma_start(out=out[a * P:(a + 1) * P, first * P:(first + count) * P], in_=res[:])
+
+        def sum_on_vector(a, first, count, picked):
+            res = keep.tile([P, count * P], F32, name=f"res_tail{first}")
+            nc.vector.tensor_tensor(out=res[:], in0=picked[:, 0, :], in1=picked[:, 1, :], op=ALU.add)
+            nc.sync.dma_start(out=out[a * P:(a + 1) * P, first * P:(first + count) * P], in_=res[:])
+
+        last = PLANES - 1
+        for a in range(last):
+            for half in range(HALVES):
+                sum_on_tensor(a, 4 * half, 4)
+        sum_on_tensor(last, 0, 2)
+        waiting = None
+        for first, count in ((2, 3), (5, 2), (7, 1)):
+            picked = gather(w_win[last], first, count)
+            if waiting is not None:
+                sum_on_vector(last, *waiting)
+            waiting = (first, count, picked)
+        sum_on_vector(last, *waiting)

@@ -106,7 +106,7 @@ def tile_attend_ggcn2_tnh_kernel(tc, dyT, w2, w1_words, w1_scales, hT, offs, out
             copy(out=u_win[a][:, cols], in_=acc[:])
 
         def gather(window, first, count):
-            picked = ring.tile([P, DEG, count * P], F32, name="picked", tag="picked", bufs=3)
+            picked = ring.tile([P, DEG, count * P], F32, name="picked", tag="picked", bufs=4)
             nc.vector.tensor_copy(
                 out=picked[:].bitcast(U32).rearrange("p j x -> p x j"),
                 in_=window.bitcast(U32).indirect(offsets[:, 16 * first:16 * (first + count)]))
@@ -120,10 +120,13 @@ def tile_attend_ggcn2_tnh_kernel(tc, dyT, w2, w1_words, w1_scales, hT, offs, out
         h_sq = [keep.tile([P, FEAT], F32, name=f"h_sq{b}", tag=f"h_sq{b}", align_bytes=64) for b in range(BLOCKS)]
 
         def square_h(b):
-            turned = psum.tile([P, PLANES, P], F32, name="turned", tag="turn")
+            turned = psum.tile([P, PLANES, P], F32, name="turned", tag="sum" if b < 4 else "turn",
+                               bufs=4 if b < 4 else 2)
             for a in range(PLANES):
                 nc.tensor.transpose(turned[:, a, :], h_raw[b // 2][:, a, (b % 2) * P:(b % 2 + 1) * P], ident[:])
-            nc.scalar.activation(out=h_sq[b][:], in_=turned[:].rearrange("p a f -> p (a f)"), func=ACT.Square)
+            squared = ring.tile([P, FEAT], F32, name="squared", bufs=3)
+            nc.scalar.activation(out=squared[:], in_=turned[:].rearrange("p a f -> p (a f)"), func=ACT.Square)
+            nc.gpsimd.tensor_scalar(out=h_sq[b][:], in0=squared[:], scalar1=-1.0, scalar2=1.0, op0=ALU.mult, op1=ALU.add)
 
         dh_cd = {}
         dh_sc = [keep.tile([P, BANK], U8, name=f"dh_sc{half}", align_bytes=64) for half in range(HALVES)]
@@ -140,9 +143,13 @@ def tile_attend_ggcn2_tnh_kernel(tc, dyT, w2, w1_words, w1_scales, hT, offs, out
 
         def through_tanh(b):
             neg = keep.tile([P, FEAT], BF16, name=f"neg_dh{b}", tag="u_all" if b == 6 else f"neg_dh{b}")
-            nc.vector.scalar_tensor_tensor(out=neg[:], in0=h_sq[b][:], scalar=1.0,
-                                           in1=su[b][:].rearrange("p a f -> p (a f)"),
-                                           op0=ALU.subtract, op1=ALU.mult)
+            sums = su[b][:].rearrange("p a f -> p (a f)")
+            if b < 6:
+                su_sb = ring.tile([P, FEAT], F32, name="su_sb", bufs=4)
+                nc.scalar.copy(out=su_sb[:], in_=sums)
+                nc.gpsimd.tensor_tensor(out=neg[:], in0=su_sb[:], in1=h_sq[b][:], op=ALU.mult)
+            else:
+                nc.vector.tensor_tensor(out=neg[:], in0=sums, in1=h_sq[b][:], op=ALU.mult)
             words = neg[:].bitcast(F32)
             back = psum.tile([P, 2, P], F32, name="back", tag="turn")
             for s in range(2):
@@ -168,9 +175,9 @@ def tile_attend_ggcn2_tnh_kernel(tc, dyT, w2, w1_words, w1_scales, hT, offs, out
                                 lhsT_scale=w1_sc[:, a * P:(a + 1) * P],
                                 rhs=dh_cd[half][:].bitcast(E5M2), rhs_scale=dh_sc[half][:], start=True, stop=True)
             if on_vector:
-                nc.vector.tensor_scalar_mul(w_win[a][:, cols], acc[:], -1.0)
+                nc.vector.tensor_copy(out=w_win[a][:, cols], in_=acc[:])
             else:
-                nc.scalar.activation(out=w_win[a][:, cols], in_=acc[:], func=ACT.Copy, scale=-1.0)
+                nc.scalar.copy(out=w_win[a][:, cols], in_=acc[:])
 
         quantise_w2(0, nc.vector.tensor_copy)
         quantise_dy(0)
@@ -180,13 +187,15 @@ def tile_attend_ggcn2_tnh_kernel(tc, dyT, w2, w1_words, w1_scales, hT, offs, out
         quantise_dy(3)
         upper(0, 1, nc.vector.tensor_copy)
 
+        for a in range(1, PLANES):
+            quantise_w2(a, nc.scalar.copy)
+            for half in range(HALVES):
+                upper(a, half, nc.scalar.copy)
+        for b in range(4):
+            square_h(b)
         for a in range(PLANES):
-            if a + 1 < PLANES:
-                quantise_w2(a + 1, nc.scalar.copy)
-                for half in range(HALVES):
-                    upper(a + 1, half, nc.scalar.copy)
             sum_upper(a, 0, 4)
-        for b in range(BLOCKS):
+        for b in range(4, BLOCKS):
             square_h(b)
         for b in range(4):
             through_tanh(b)

@@ -34,7 +34,7 @@ def tile_attend_ggcn2_tnh_kernel(tc, dyT, w2, w1_words, w1_scales, hT, offs, out
     with ExitStack() as ctx:
         keep = ctx.enter_context(tc.tile_pool(name="keep", bufs=1))
         ring = ctx.enter_context(tc.tile_pool(name="ring", bufs=2))
-        psum = ctx.enter_context(tc.psum_pool(name="psum", bufs=2))
+        psum = ctx.enter_context(tc.psum_pool(name="psum", bufs=1))
 
         offsets = keep.tile([P, NODES * DEG // 16], U16, name="offsets")
         ident = keep.tile([P, P], F32, name="ident")
@@ -56,7 +56,6 @@ def tile_attend_ggcn2_tnh_kernel(tc, dyT, w2, w1_words, w1_scales, hT, offs, out
         nc.sync.dma_start(offsets[:], offs)
         w2_rest = load("w2_rest", w2_rows[:, :, 2 * P:FEAT], 2 * P)
         h_raw = [load(f"h_raw{c}", h_rows[:, :, c * 2 * P:(c + 1) * 2 * P], 2 * P) for c in range(BLOCKS // 2)]
-        w2_raw = [w2_first[:], w2_second[:], w2_rest[:, :, 0:P], w2_rest[:, :, P:2 * P]]
 
         u_all = keep.tile([P, (PLANES - 1) * NODES + WINDOW], F32, name="u_all", tag="u_all")
         w_all = keep.tile([P, (PLANES - 1) * NODES + WINDOW], F32, name="w_all")
@@ -75,13 +74,15 @@ def tile_attend_ggcn2_tnh_kernel(tc, dyT, w2, w1_words, w1_scales, hT, offs, out
         def interleave(copy, dst, src):
             copy(out=dst.rearrange("p (c i) t -> p c t i", i=4), in_=src.rearrange("p t (c i) -> p c t i", i=4))
 
-        w2_cd = [keep.tile([P, P], U32, name=f"w2_cd{a}", align_bytes=64) for a in range(PLANES)]
-        w2_sc = [keep.tile([P, P], U8, name=f"w2_sc{a}", align_bytes=64) for a in range(PLANES)]
+        w2_cd = keep.tile([P, FEAT], U32, name="w2_cd", align_bytes=64)
+        w2_sc = keep.tile([P, FEAT], U8, name="w2_sc", align_bytes=64)
 
-        def quantise_w2(a, copy):
-            grouped = keep.tile([P, P, PACK], BF16, name=f"w2_bf{a}", align_bytes=64)
-            interleave(copy, grouped[:], w2_raw[a])
-            nc.vector.quantize_mx(out=w2_cd[a][:].bitcast(E4M3), scales=w2_sc[a][:],
+        def quantise_w2(f0, raw, copy):
+            width = raw.shape[2]
+            grouped = keep.tile([P, width, PACK], BF16, name=f"w2_bf{f0}", align_bytes=64)
+            interleave(copy, grouped[:], raw)
+            cols = slice(f0, f0 + width)
+            nc.vector.quantize_mx(out=w2_cd[:, cols].bitcast(E4M3), scales=w2_sc[:, cols],
                                   in_=grouped[:].rearrange("p c t -> p (c t)"))
 
         dy_cd = keep.tile([P, NODES], U32, name="dy_cd", align_bytes=64)
@@ -100,13 +101,17 @@ def tile_attend_ggcn2_tnh_kernel(tc, dyT, w2, w1_words, w1_scales, hT, offs, out
 
         def upper(a, half, copy):
             cols = slice(half * BANK, (half + 1) * BANK)
-            acc = psum.tile([P, BANK], F32, name="acc", tag="mm")
-            nc.tensor.matmul_mx(out=acc[:], lhsT=w2_cd[a][:].bitcast(E4M3), lhsT_scale=w2_sc[a][:],
+            acc = psum.tile([P, BANK], F32, name="acc", tag="GH"[half])
+            nc.tensor.matmul_mx(out=acc[:], lhsT=w2_cd[:, a * P:(a + 1) * P].bitcast(E4M3),
+                                lhsT_scale=w2_sc[:, a * P:(a + 1) * P],
                                 rhs=dy_cd[:, cols].bitcast(E5M2), rhs_scale=dy_sc[:, cols], start=True, stop=True)
             copy(out=u_win[a][:, cols], in_=acc[:])
 
-        def gather(window, first, count):
-            picked = ring.tile([P, DEG, count * P], F32, name="picked", tag="picked", bufs=4)
+        def gather(window, first, count, after=None):
+            if after is None:
+                picked = ring.tile([P, DEG, count * P], F32, name="picked", tag="picked", bufs=7)
+            else:
+                picked = keep.tile([P, DEG, count * P], F32, name="picked", tag=after, align_bytes=64)
             nc.vector.tensor_copy(
                 out=picked[:].bitcast(U32).rearrange("p j x -> p x j"),
                 in_=window.bitcast(U32).indirect(offsets[:, 16 * first:16 * (first + count)]))
@@ -120,13 +125,14 @@ def tile_attend_ggcn2_tnh_kernel(tc, dyT, w2, w1_words, w1_scales, hT, offs, out
         h_sq = [keep.tile([P, FEAT], F32, name=f"h_sq{b}", tag=f"h_sq{b}", align_bytes=64) for b in range(BLOCKS)]
 
         def square_h(b):
-            turned = psum.tile([P, PLANES, P], F32, name="turned", tag="sum" if b < 4 else "turn",
-                               bufs=4 if b < 4 else 2)
+            turned = psum.tile([P, PLANES, P], F32, name="turned", tag="ABCDEFGH"[b])
             for a in range(PLANES):
                 nc.tensor.transpose(turned[:, a, :], h_raw[b // 2][:, a, (b % 2) * P:(b % 2 + 1) * P], ident[:])
-            squared = ring.tile([P, FEAT], F32, name="squared", bufs=3)
+            squared = keep.tile([P, FEAT], F32, name="squared", tag=f"squared{b}", align_bytes=64) if b < 6 else h_sq[b]
             nc.scalar.activation(out=squared[:], in_=turned[:].rearrange("p a f -> p (a f)"), func=ACT.Square)
-            nc.gpsimd.tensor_scalar(out=h_sq[b][:], in0=squared[:], scalar1=-1.0, scalar2=1.0, op0=ALU.mult, op1=ALU.add)
+            if b < 6:
+                nc.gpsimd.tensor_scalar(out=h_sq[b][:], in0=squared[:], scalar1=1.0, scalar2=-1.0,
+                                        op0=ALU.mult, op1=ALU.add)
 
         dh_cd = {}
         dh_sc = [keep.tile([P, BANK], U8, name=f"dh_sc{half}", align_bytes=64) for half in range(HALVES)]
@@ -134,30 +140,37 @@ def tile_attend_ggcn2_tnh_kernel(tc, dyT, w2, w1_words, w1_scales, hT, offs, out
         groups = ((0, 4), (4, 2), (6, 1), (7, 1))
         dh_bf = [keep.tile([P, count * P * PACK], BF16, name=f"dh_bf{first}", align_bytes=64) for first, count in groups]
 
-        def sum_upper(a, first, count):
-            picked = gather(u_win[a], first, count)
+        def sum_upper(a, first, count, after=None):
+            picked = gather(u_win[a], first, count, after)
             for k in range(count):
                 if a == 0:
-                    su[first + k] = psum.tile([P, PLANES, P], F32, name="su", tag="sum", bufs=4)
+                    su[first + k] = psum.tile([P, PLANES, P], F32, name="su", tag="ABCDABCE"[first + k])
                 sum_turned(su[first + k][:, a, :], picked, k)
 
+        neg = {}
+
         def through_tanh(b):
-            neg = keep.tile([P, FEAT], BF16, name=f"neg_dh{b}", tag="u_all" if b == 6 else f"neg_dh{b}")
+            neg[b] = keep.tile([P, FEAT], BF16, name=f"neg_dh{b}")
             sums = su[b][:].rearrange("p a f -> p (a f)")
             if b < 6:
-                su_sb = ring.tile([P, FEAT], F32, name="su_sb", bufs=4)
+                su_sb = keep.tile([P, FEAT], F32, name="su_sb", tag=f"su_sb{b}", align_bytes=64)
                 nc.scalar.copy(out=su_sb[:], in_=sums)
-                nc.gpsimd.tensor_tensor(out=neg[:], in0=su_sb[:], in1=h_sq[b][:], op=ALU.mult)
+                nc.gpsimd.tensor_tensor(out=neg[b][:], in0=su_sb[:], in1=h_sq[b][:], op=ALU.mult)
             else:
-                nc.vector.tensor_tensor(out=neg[:], in0=sums, in1=h_sq[b][:], op=ALU.mult)
-            words = neg[:].bitcast(F32)
-            back = psum.tile([P, 2, P], F32, name="back", tag="turn")
-            for s in range(2):
-                nc.tensor.transpose(back[:, s, :], words[:, s::2], ident[:])
-            g = max(i for i, (first, count) in enumerate(groups) if first <= b)
-            k = b - groups[g][0]
-            nc.scalar.copy(out=dh_bf[g][:].bitcast(F32)[:, 2 * P * k:2 * P * (k + 1)].rearrange("p (x s) -> p x s", s=2),
-                           in_=back[:].rearrange("p s x -> p x s"))
+                nc.vector.scalar_tensor_tensor(out=neg[b][:], in0=h_sq[b][:], scalar=1.0, in1=sums,
+                                               op0=ALU.subtract, op1=ALU.mult)
+
+        def turn_back(first, count, bank):
+            back = psum.tile([P, 2, count * P], F32, name="back", tag=bank)
+            for k in range(count):
+                words = neg[first + k][:].bitcast(F32)
+                for s in range(2):
+                    nc.tensor.transpose(back[:, s, k * P:(k + 1) * P], words[:, s::2], ident[:])
+            g = max(i for i, group in enumerate(groups) if group[0] <= first)
+            k0 = first - groups[g][0]
+            nc.scalar.copy(
+                out=dh_bf[g][:].bitcast(F32)[:, 2 * P * k0:2 * P * (k0 + count)].rearrange("p (x s) -> p x s", s=2),
+                in_=back[:].rearrange("p s x -> p x s"))
 
         def quantise_dh(g):
             first, count = groups[g]
@@ -170,16 +183,17 @@ def tile_attend_ggcn2_tnh_kernel(tc, dyT, w2, w1_words, w1_scales, hT, offs, out
 
         def lower(a, half, on_vector):
             cols = slice(half * BANK, (half + 1) * BANK)
-            acc = psum.tile([P, BANK], F32, name="acc", tag="mm")
+            acc = psum.tile([P, BANK], F32, name="acc", tag="GH"[half])
             nc.tensor.matmul_mx(out=acc[:], lhsT=w1_cd[:, 2 * a * P:2 * (a + 1) * P].bitcast(E2M1),
                                 lhsT_scale=w1_sc[:, a * P:(a + 1) * P],
                                 rhs=dh_cd[half][:].bitcast(E5M2), rhs_scale=dh_sc[half][:], start=True, stop=True)
             if on_vector:
-                nc.vector.tensor_copy(out=w_win[a][:, cols], in_=acc[:])
+                nc.vector.tensor_scalar_mul(w_win[a][:, cols], acc[:], -1.0)
             else:
-                nc.scalar.copy(out=w_win[a][:, cols], in_=acc[:])
+                nc.scalar.activation(out=w_win[a][:, cols], in_=acc[:], func=ACT.Copy, scale=-1.0)
 
-        quantise_w2(0, nc.vector.tensor_copy)
+        w2_raw = [w2_first[:], w2_second[:], w2_rest[:, :, 0:P], w2_rest[:, :, P:2 * P]]
+        quantise_w2(0, w2_raw[0], nc.vector.tensor_copy)
         quantise_dy(0)
         quantise_dy(1)
         upper(0, 0, nc.scalar.copy)
@@ -188,23 +202,35 @@ def tile_attend_ggcn2_tnh_kernel(tc, dyT, w2, w1_words, w1_scales, hT, offs, out
         upper(0, 1, nc.vector.tensor_copy)
 
         for a in range(1, PLANES):
-            quantise_w2(a, nc.scalar.copy)
+            quantise_w2(a * P, w2_raw[a], nc.scalar.copy)
             for half in range(HALVES):
                 upper(a, half, nc.scalar.copy)
         for b in range(4):
             square_h(b)
-        for a in range(PLANES):
+        for a in range(PLANES - 1):
             sum_upper(a, 0, 4)
+        sum_upper(PLANES - 1, 0, 2)
+        sum_upper(PLANES - 1, 2, 2)
         for b in range(4, BLOCKS):
             square_h(b)
         for b in range(4):
             through_tanh(b)
+        turn_back(0, 2, "D")
         for a in range(PLANES):
-            sum_upper(a, 4, 3)
-        for a in range(PLANES):
-            sum_upper(a, 7, 1)
-        for b in range(4, BLOCKS):
-            through_tanh(b)
+            sum_upper(a, 4, 2, f"squared{a}" if a < PLANES - 1 else None)
+        through_tanh(4)
+        through_tanh(5)
+        turn_back(2, 2, "B")
+        turn_back(4, 2, "D")
+        sum_upper(0, 6, 2, "su_sb0")
+        sum_upper(1, 6, 2, "su_sb1")
+        sum_upper(2, 6, 2, "su_sb2")
+        sum_upper(3, 6, 1, "su_sb3")
+        sum_upper(3, 7, 1, "h_sq3")
+        through_tanh(6)
+        turn_back(6, 1, "F")
+        through_tanh(7)
+        turn_back(7, 1, "C")
         quantise_dh(0)
         lower(0, 0, False)
         for g in range(1, len(groups)):
@@ -214,34 +240,13 @@ def tile_attend_ggcn2_tnh_kernel(tc, dyT, w2, w1_words, w1_scales, hT, offs, out
             for half in range(HALVES):
                 lower(a, half, False)
 
-        def sum_on_tensor(a, first, count):
-            so = psum.tile([P, count, P], F32, name="so", tag="sum", bufs=4)
+        pieces = [(a, first, 4) for a in range(PLANES - 1) for first in (0, 4)]
+        pieces += [(PLANES - 1, 0, 4), (PLANES - 1, 4, 2), (PLANES - 1, 6, 1), (PLANES - 1, 7, 1)]
+        for i, (a, first, count) in enumerate(pieces):
             picked = gather(w_win[a], first, count)
-            for k in range(count):
-                sum_turned(so[:, k, :], picked, k)
-            so_sb = ring.tile([P, count, P], F32, name="so_sb")
-            nc.scalar.copy(out=so_sb[:], in_=so[:])
-            upright = psum.tile([P, count, P], F32, name="upright", tag="turn")
-            for k in range(count):
-                nc.tensor.transpose(upright[:, k, :], so_sb[:, k, :], ident[:])
-            res = ring.tile([P, count * P], F32, name="res", bufs=4)
-            nc.scalar.copy(out=res[:], in_=upright[:].rearrange("p k x -> p (k x)"))
-            nc.scalar.dma_start(out=out[a * P:(a + 1) * P, first * P:(first + count) * P], in_=res[:])
-
-        def sum_on_vector(a, first, count, picked):
-            res = keep.tile([P, count * P], F32, name=f"res_tail{first}")
-            nc.vector.tensor_tensor(out=res[:], in0=picked[:, 0, :], in1=picked[:, 1, :], op=ALU.add)
-            nc.sync.dma_start(out=out[a * P:(a + 1) * P, first * P:(first + count) * P], in_=res[:])
-
-        last = PLANES - 1
-        for a in range(last):
-            for half in range(HALVES):
-                sum_on_tensor(a, 4 * half, 4)
-        sum_on_tensor(last, 0, 2)
-        waiting = None
-        for first, count in ((2, 3), (5, 2), (7, 1)):
-            picked = gather(w_win[last], first, count)
-            if waiting is not None:
-                sum_on_vector(last, *waiting)
-            waiting = (first, count, picked)
-        sum_on_vector(last, *waiting)
+            res = keep.tile([P, count * P], F32, name=f"res{i}")
+            final = i == len(pieces) - 1
+            adder = nc.vector if final else nc.gpsimd
+            adder.tensor_tensor(out=res[:], in0=picked[:, 0, :], in1=picked[:, 1, :], op=ALU.add)
+            queue = nc.scalar if final else nc.sync
+            queue.dma_start(out=out[a * P:(a + 1) * P, first * P:(first + count) * P], in_=res[:])

@@ -24,47 +24,58 @@ PLANES = FEAT // P
 BLOCKS = NODES // P
 BANK = 512
 HALVES = NODES // BANK
-DY_CHUNKS = ((0, 256), (256, 256), (512, 256), (768, 256))
+HALF_BLOCKS = BANK // P
+LIST_ROWS = 16
+BLOCK_COLUMNS = P * DEG // LIST_ROWS
+ALIGN = 64
+DY_CHUNK = 256
+VECTOR_CAST = 144
 WINDOW = 1376
+PICKED_BUFS = 7
+GPSIMD_PRODUCTS = 5
+GPSIMD_SHIFTS = 4
+DH_GROUPS = ((0, 4), (4, 2), (6, 1), (7, 1))
 FLOPS = 2 * 2 * FEAT * FEAT * NODES
 
 
 def tile_attend_ggcn2_tnh_kernel(tc, dyT, w2, w1_words, w1_scales, hT, offs, out):
     nc = tc.nc
+    last_plane = PLANES - 1
     with ExitStack() as ctx:
         keep = ctx.enter_context(tc.tile_pool(name="keep", bufs=1))
         ring = ctx.enter_context(tc.tile_pool(name="ring", bufs=2))
         psum = ctx.enter_context(tc.psum_pool(name="psum", bufs=1))
 
-        offsets = keep.tile([P, NODES * DEG // 16], U16, name="offsets")
+        offsets = keep.tile([P, NODES * DEG // LIST_ROWS], U16, name="offsets")
         ident = keep.tile([P, P], F32, name="ident")
-        w1_sc = keep.tile([P, FEAT], U8, name="w1_sc", align_bytes=64)
-        w1_cd = keep.tile([P, 2 * FEAT], U8, name="w1_cd", align_bytes=64)
+        w1_sc = keep.tile([P, FEAT], U8, name="w1_sc", align_bytes=ALIGN)
+        w1_cd = keep.tile([P, 2 * FEAT], U8, name="w1_cd", align_bytes=ALIGN)
 
-        w2_rows = w2.rearrange("(p j) f -> p j f", j=PACK)
-        dy_rows = dyT.rearrange("(p j) x -> p j x", j=PACK)
+        w2_rows = w2.rearrange("(p t) f -> p t f", t=PACK)
+        dy_rows = dyT.rearrange("(p t) x -> p t x", t=PACK)
         h_rows = hT.rearrange("(a p) x -> p a x", p=P)
 
         def load(name, src, width):
-            t = keep.tile([P, PACK, width], F32, name=name)
-            nc.sync.dma_start(out=t[:], in_=src)
-            return t
+            raw = keep.tile([P, src.shape[1], width], F32, name=name)
+            nc.sync.dma_start(out=raw[:], in_=src)
+            return raw
 
         w2_first = load("w2_first", w2_rows[:, :, 0:P], P)
-        dy_raw = [load(f"dy_raw{x0}", dy_rows[:, :, x0:x0 + n], n) for x0, n in DY_CHUNKS]
+        dy_raw = [load(f"dy_raw{x0}", dy_rows[:, :, x0:x0 + DY_CHUNK], DY_CHUNK) for x0 in range(0, NODES, DY_CHUNK)]
         w2_second = load("w2_second", w2_rows[:, :, P:2 * P], P)
         nc.sync.dma_start(offsets[:], offs)
         w2_rest = load("w2_rest", w2_rows[:, :, 2 * P:FEAT], 2 * P)
         h_raw = [load(f"h_raw{c}", h_rows[:, :, c * 2 * P:(c + 1) * 2 * P], 2 * P) for c in range(BLOCKS // 2)]
 
-        u_all = keep.tile([P, (PLANES - 1) * NODES + WINDOW], F32, name="u_all", tag="u_all")
-        w_all = keep.tile([P, (PLANES - 1) * NODES + WINDOW], F32, name="w_all")
+        u_all = keep.tile([P, last_plane * NODES + WINDOW], F32, name="u_all")
+        w_all = keep.tile([P, last_plane * NODES + WINDOW], F32, name="w_all")
         for table in (u_all, w_all):
             nc.vector.memset(table[:, PLANES * NODES:], 0.0)
-        starts = [(PLANES - 1 - a) * NODES for a in range(PLANES)]
-        u_win = [u_all[:, s:s + WINDOW] for s in starts]
-        w_win = [w_all[:, s:s + WINDOW] for s in starts]
+        starts = [(last_plane - a) * NODES for a in range(PLANES)]
+        u_win = [u_all[:, start:start + WINDOW] for start in starts]
+        w_win = [w_all[:, start:start + WINDOW] for start in starts]
         make_identity(nc, ident[:])
+
         nc.gpsimd.memset(w1_sc[:].bitcast(U32), 0)
         nc.sync.dma_start(out=w1_cd[:].bitcast(I32), in_=w1_words[0].bitcast(I32))
         for q in range(4):
@@ -74,32 +85,29 @@ def tile_attend_ggcn2_tnh_kernel(tc, dyT, w2, w1_words, w1_scales, hT, offs, out
         def interleave(copy, dst, src):
             copy(out=dst.rearrange("p (c i) t -> p c t i", i=4), in_=src.rearrange("p t (c i) -> p c t i", i=4))
 
-        w2_cd = keep.tile([P, FEAT], U32, name="w2_cd", align_bytes=64)
-        w2_sc = keep.tile([P, FEAT], U8, name="w2_sc", align_bytes=64)
+        w2_cd = keep.tile([P, FEAT], U32, name="w2_cd", align_bytes=ALIGN)
+        w2_sc = keep.tile([P, FEAT], U8, name="w2_sc", align_bytes=ALIGN)
+        w2_raw = [w2_first[:], w2_second[:], w2_rest[:, :, 0:P], w2_rest[:, :, P:2 * P]]
 
-        def quantise_w2(f0, raw, copy):
-            width = raw.shape[2]
-            grouped = keep.tile([P, width, PACK], BF16, name=f"w2_bf{f0}", align_bytes=64)
-            interleave(copy, grouped[:], raw)
-            cols = slice(f0, f0 + width)
+        def quantise_w2(a, copy):
+            grouped = keep.tile([P, P, PACK], BF16, name=f"w2_bf{a * P}", align_bytes=ALIGN)
+            interleave(copy, grouped[:], w2_raw[a])
+            cols = slice(a * P, (a + 1) * P)
             nc.vector.quantize_mx(out=w2_cd[:, cols].bitcast(E4M3), scales=w2_sc[:, cols],
                                   in_=grouped[:].rearrange("p c t -> p (c t)"))
 
-        dy_cd = keep.tile([P, NODES], U32, name="dy_cd", align_bytes=64)
-        dy_sc = keep.tile([P, NODES], U8, name="dy_sc", align_bytes=64)
+        dy_cd = keep.tile([P, NODES], U32, name="dy_cd", align_bytes=ALIGN)
+        dy_sc = keep.tile([P, NODES], U8, name="dy_sc", align_bytes=ALIGN)
 
         def quantise_dy(c):
-            x0, n = DY_CHUNKS[c]
-            cut = 9 * n // 16
-            grouped = keep.tile([P, n, PACK], BF16, name=f"dy_bf{c}", align_bytes=64)
-            interleave(nc.scalar.copy, grouped[:, cut:, :], dy_raw[c][:, :, cut:])
-            interleave(nc.vector.tensor_copy, grouped[:, :cut, :], dy_raw[c][:, :, :cut])
-            cols = slice(x0, x0 + n)
+            grouped = keep.tile([P, DY_CHUNK, PACK], BF16, name=f"dy_bf{c}", align_bytes=ALIGN)
+            interleave(nc.scalar.copy, grouped[:, VECTOR_CAST:, :], dy_raw[c][:, :, VECTOR_CAST:])
+            interleave(nc.vector.tensor_copy, grouped[:, :VECTOR_CAST, :], dy_raw[c][:, :, :VECTOR_CAST])
+            cols = slice(c * DY_CHUNK, (c + 1) * DY_CHUNK)
             nc.vector.quantize_mx(out=dy_cd[:, cols].bitcast(E5M2), scales=dy_sc[:, cols],
                                   in_=grouped[:].rearrange("p c t -> p (c t)"))
 
-
-        def upper(a, half, copy):
+        def upper_product(a, half, copy):
             cols = slice(half * BANK, (half + 1) * BANK)
             acc = psum.tile([P, BANK], F32, name="acc", tag="GH"[half])
             nc.tensor.matmul_mx(out=acc[:], lhsT=w2_cd[:, a * P:(a + 1) * P].bitcast(E4M3),
@@ -107,81 +115,85 @@ def tile_attend_ggcn2_tnh_kernel(tc, dyT, w2, w1_words, w1_scales, hT, offs, out
                                 rhs=dy_cd[:, cols].bitcast(E5M2), rhs_scale=dy_sc[:, cols], start=True, stop=True)
             copy(out=u_win[a][:, cols], in_=acc[:])
 
-        def gather(window, first, count, after=None):
-            if after is None:
-                picked = ring.tile([P, DEG, count * P], F32, name="picked", tag="picked", bufs=7)
+        def look_up(window, first, count, reuse=None):
+            if reuse is None:
+                picked = ring.tile([P, DEG, count * P], F32, name="picked", tag="picked", bufs=PICKED_BUFS)
             else:
-                picked = keep.tile([P, DEG, count * P], F32, name="picked", tag=after, align_bytes=64)
-            nc.vector.tensor_copy(
-                out=picked[:].bitcast(U32).rearrange("p j x -> p x j"),
-                in_=window.bitcast(U32).indirect(offsets[:, 16 * first:16 * (first + count)]))
+                picked = keep.tile([P, DEG, count * P], F32, name="picked", tag=reuse, align_bytes=ALIGN)
+            entries = offsets[:, BLOCK_COLUMNS * first:BLOCK_COLUMNS * (first + count)]
+            nc.vector.tensor_copy(out=picked[:].bitcast(U32).rearrange("p j x -> p x j"),
+                                  in_=window.bitcast(U32).indirect(entries))
             return picked
 
-        def sum_turned(dst, picked, k):
-            for j in range(DEG):
-                nc.tensor.matmul(dst, picked[:, j, k * P:(k + 1) * P], ident[:], is_transpose=True,
-                                 start=(j == 0), stop=(j == DEG - 1))
+        h_term = [keep.tile([P, FEAT], F32, name=f"h_term{b}", tag=f"h_term{b}", align_bytes=ALIGN)
+                  for b in range(BLOCKS)]
 
-        h_sq = [keep.tile([P, FEAT], F32, name=f"h_sq{b}", tag=f"h_sq{b}", align_bytes=64) for b in range(BLOCKS)]
-
-        def square_h(b):
+        def make_h_term(b):
             turned = psum.tile([P, PLANES, P], F32, name="turned", tag="ABCDEFGH"[b])
             for a in range(PLANES):
                 nc.tensor.transpose(turned[:, a, :], h_raw[b // 2][:, a, (b % 2) * P:(b % 2 + 1) * P], ident[:])
-            squared = keep.tile([P, FEAT], F32, name="squared", tag=f"squared{b}", align_bytes=64) if b < 6 else h_sq[b]
-            nc.scalar.activation(out=squared[:], in_=turned[:].rearrange("p a f -> p (a f)"), func=ACT.Square)
-            if b < 6:
-                nc.gpsimd.tensor_scalar(out=h_sq[b][:], in0=squared[:], scalar1=1.0, scalar2=-1.0,
+            turned_row = turned[:].rearrange("p a f -> p (a f)")
+            if b >= GPSIMD_PRODUCTS:
+                nc.scalar.activation(out=h_term[b][:], in_=turned_row, func=ACT.Square)
+                return
+            squared = keep.tile([P, FEAT], F32, name="squared", tag=f"squared{b}", align_bytes=ALIGN)
+            nc.scalar.activation(out=squared[:], in_=turned_row, func=ACT.Square)
+            if b < GPSIMD_SHIFTS:
+                nc.gpsimd.tensor_scalar(out=h_term[b][:], in0=squared[:], scalar1=1.0, scalar2=-1.0,
                                         op0=ALU.mult, op1=ALU.add)
+            else:
+                nc.scalar.activation(out=h_term[b][:], in_=squared[:], func=ACT.Copy, scale=1.0, bias=-1.0)
 
         dh_cd = {}
-        dh_sc = [keep.tile([P, BANK], U8, name=f"dh_sc{half}", align_bytes=64) for half in range(HALVES)]
+        dh_sc = [keep.tile([P, BANK], U8, name=f"dh_sc{half}", align_bytes=ALIGN) for half in range(HALVES)]
+        dh_bf = [keep.tile([P, count * P * PACK], BF16, name=f"dh_bf{first}", align_bytes=ALIGN)
+                 for first, count in DH_GROUPS]
         su = {}
-        groups = ((0, 4), (4, 2), (6, 1), (7, 1))
-        dh_bf = [keep.tile([P, count * P * PACK], BF16, name=f"dh_bf{first}", align_bytes=64) for first, count in groups]
+        minus_dh = {}
+        su_banks = "ABCDABCE"
 
-        def sum_upper(a, first, count, after=None):
-            picked = gather(u_win[a], first, count, after)
+        def first_sum(a, first, count, reuse=None):
+            picked = look_up(u_win[a], first, count, reuse)
             for k in range(count):
                 if a == 0:
-                    su[first + k] = psum.tile([P, PLANES, P], F32, name="su", tag="ABCDABCE"[first + k])
-                sum_turned(su[first + k][:, a, :], picked, k)
-
-        neg = {}
+                    su[first + k] = psum.tile([P, PLANES, P], F32, name="su", tag=su_banks[first + k])
+                for j in range(DEG):
+                    nc.tensor.matmul(su[first + k][:, a, :], picked[:, j, k * P:(k + 1) * P], ident[:],
+                                     is_transpose=True, start=(j == 0), stop=(j == DEG - 1))
 
         def through_tanh(b):
-            neg[b] = keep.tile([P, FEAT], BF16, name=f"neg_dh{b}")
+            minus_dh[b] = keep.tile([P, FEAT], BF16, name=f"minus_dh{b}")
             sums = su[b][:].rearrange("p a f -> p (a f)")
-            if b < 6:
-                su_sb = keep.tile([P, FEAT], F32, name="su_sb", tag=f"su_sb{b}", align_bytes=64)
+            if b < GPSIMD_PRODUCTS:
+                su_sb = keep.tile([P, FEAT], F32, name="su_sb", tag=f"su_sb{b}", align_bytes=ALIGN)
                 nc.scalar.copy(out=su_sb[:], in_=sums)
-                nc.gpsimd.tensor_tensor(out=neg[b][:], in0=su_sb[:], in1=h_sq[b][:], op=ALU.mult)
+                nc.gpsimd.tensor_tensor(out=minus_dh[b][:], in0=su_sb[:], in1=h_term[b][:], op=ALU.mult)
             else:
-                nc.vector.scalar_tensor_tensor(out=neg[b][:], in0=h_sq[b][:], scalar=1.0, in1=sums,
+                nc.vector.scalar_tensor_tensor(out=minus_dh[b][:], in0=h_term[b][:], scalar=1.0, in1=sums,
                                                op0=ALU.subtract, op1=ALU.mult)
 
         def turn_back(first, count, bank):
             back = psum.tile([P, 2, count * P], F32, name="back", tag=bank)
             for k in range(count):
-                words = neg[first + k][:].bitcast(F32)
+                words = minus_dh[first + k][:].bitcast(F32)
                 for s in range(2):
                     nc.tensor.transpose(back[:, s, k * P:(k + 1) * P], words[:, s::2], ident[:])
-            g = max(i for i, group in enumerate(groups) if group[0] <= first)
-            k0 = first - groups[g][0]
-            nc.scalar.copy(
-                out=dh_bf[g][:].bitcast(F32)[:, 2 * P * k0:2 * P * (k0 + count)].rearrange("p (x s) -> p x s", s=2),
-                in_=back[:].rearrange("p s x -> p x s"))
+            g = max(i for i, group in enumerate(DH_GROUPS) if group[0] <= first)
+            k0 = first - DH_GROUPS[g][0]
+            dst = dh_bf[g][:].bitcast(F32)[:, 2 * P * k0:2 * P * (k0 + count)]
+            nc.scalar.copy(out=dst.rearrange("p (x s) -> p x s", s=2), in_=back[:].rearrange("p s x -> p x s"))
 
         def quantise_dh(g):
-            first, count = groups[g]
-            half, k = divmod(first, 4)
+            first, count = DH_GROUPS[g]
+            half, k = divmod(first, HALF_BLOCKS)
             if k == 0:
-                dh_cd[half] = keep.tile([P, BANK], U32, name=f"dh_cd{half}", align_bytes=64,
-                                        tag="h_sq7" if half == 0 else "dh_cd1")
+                dh_cd[half] = keep.tile([P, BANK], U32, name=f"dh_cd{half}", align_bytes=ALIGN,
+                                        tag=f"h_term{BLOCKS - 1}" if half == 0 else "dh_cd1")
             cols = slice(k * P, (k + count) * P)
-            nc.vector.quantize_mx(out=dh_cd[half][:, cols].bitcast(E5M2), scales=dh_sc[half][:, cols], in_=dh_bf[g][:])
+            nc.vector.quantize_mx(out=dh_cd[half][:, cols].bitcast(E5M2), scales=dh_sc[half][:, cols],
+                                  in_=dh_bf[g][:])
 
-        def lower(a, half, on_vector):
+        def lower_product(a, half, on_vector):
             cols = slice(half * BANK, (half + 1) * BANK)
             acc = psum.tile([P, BANK], F32, name="acc", tag="GH"[half])
             nc.tensor.matmul_mx(out=acc[:], lhsT=w1_cd[:, 2 * a * P:2 * (a + 1) * P].bitcast(E2M1),
@@ -192,61 +204,61 @@ def tile_attend_ggcn2_tnh_kernel(tc, dyT, w2, w1_words, w1_scales, hT, offs, out
             else:
                 nc.scalar.activation(out=w_win[a][:, cols], in_=acc[:], func=ACT.Copy, scale=-1.0)
 
-        w2_raw = [w2_first[:], w2_second[:], w2_rest[:, :, 0:P], w2_rest[:, :, P:2 * P]]
-        quantise_w2(0, w2_raw[0], nc.vector.tensor_copy)
-        quantise_dy(0)
-        quantise_dy(1)
-        upper(0, 0, nc.scalar.copy)
-        quantise_dy(2)
-        quantise_dy(3)
-        upper(0, 1, nc.vector.tensor_copy)
+        chunks_in_half = BANK // DY_CHUNK
+        quantise_w2(0, nc.vector.tensor_copy)
+        for half in range(HALVES):
+            for c in range(half * chunks_in_half, (half + 1) * chunks_in_half):
+                quantise_dy(c)
+            upper_product(0, half, nc.vector.tensor_copy if half == HALVES - 1 else nc.scalar.copy)
 
         for a in range(1, PLANES):
-            quantise_w2(a * P, w2_raw[a], nc.scalar.copy)
+            quantise_w2(a, nc.scalar.copy)
             for half in range(HALVES):
-                upper(a, half, nc.scalar.copy)
-        for b in range(4):
-            square_h(b)
-        for a in range(PLANES - 1):
-            sum_upper(a, 0, 4)
-        sum_upper(PLANES - 1, 0, 2)
-        sum_upper(PLANES - 1, 2, 2)
-        for b in range(4, BLOCKS):
-            square_h(b)
-        for b in range(4):
+                upper_product(a, half, nc.scalar.copy)
+        for b in range(HALF_BLOCKS):
+            make_h_term(b)
+        for a in range(last_plane):
+            first_sum(a, 0, HALF_BLOCKS)
+        first_sum(last_plane, 0, 2)
+        first_sum(last_plane, 2, 2)
+        for b in range(HALF_BLOCKS):
             through_tanh(b)
+        for b in range(HALF_BLOCKS, BLOCKS):
+            make_h_term(b)
         turn_back(0, 2, "D")
+
         for a in range(PLANES):
-            sum_upper(a, 4, 2, f"squared{a}" if a < PLANES - 1 else None)
+            first_sum(a, 4, 2, f"squared{a}" if a < last_plane else None)
         through_tanh(4)
         through_tanh(5)
         turn_back(2, 2, "B")
         turn_back(4, 2, "D")
-        sum_upper(0, 6, 2, "su_sb0")
-        sum_upper(1, 6, 2, "su_sb1")
-        sum_upper(2, 6, 2, "su_sb2")
-        sum_upper(3, 6, 1, "su_sb3")
-        sum_upper(3, 7, 1, "h_sq3")
+
+        for a in range(last_plane):
+            first_sum(a, 6, 2, f"su_sb{a}")
+        first_sum(last_plane, 6, 1, f"su_sb{last_plane}")
+        first_sum(last_plane, 7, 1, f"h_term{last_plane}")
         through_tanh(6)
         turn_back(6, 1, "F")
         through_tanh(7)
         turn_back(7, 1, "C")
+
         quantise_dh(0)
-        lower(0, 0, False)
-        for g in range(1, len(groups)):
+        lower_product(0, 0, on_vector=False)
+        for g in range(1, len(DH_GROUPS)):
             quantise_dh(g)
-        lower(0, 1, True)
+        lower_product(0, 1, on_vector=True)
         for a in range(1, PLANES):
             for half in range(HALVES):
-                lower(a, half, False)
+                lower_product(a, half, on_vector=False)
 
-        pieces = [(a, first, 4) for a in range(PLANES - 1) for first in (0, 4)]
-        pieces += [(PLANES - 1, 0, 4), (PLANES - 1, 4, 2), (PLANES - 1, 6, 1), (PLANES - 1, 7, 1)]
+        pieces = [(a, first, HALF_BLOCKS) for a in range(last_plane) for first in (0, HALF_BLOCKS)]
+        pieces += [(last_plane, 0, 4), (last_plane, 4, 2), (last_plane, 6, 1), (last_plane, 7, 1)]
         for i, (a, first, count) in enumerate(pieces):
-            picked = gather(w_win[a], first, count)
-            res = keep.tile([P, count * P], F32, name=f"res{i}")
-            final = i == len(pieces) - 1
-            adder = nc.vector if final else nc.gpsimd
-            adder.tensor_tensor(out=res[:], in0=picked[:, 0, :], in1=picked[:, 1, :], op=ALU.add)
-            queue = nc.scalar if final else nc.sync
-            queue.dma_start(out=out[a * P:(a + 1) * P, first * P:(first + count) * P], in_=res[:])
+            picked = look_up(w_win[a], first, count)
+            result = keep.tile([P, count * P], F32, name=f"res{i}")
+            is_last = i == len(pieces) - 1
+            adder = nc.vector if is_last else nc.gpsimd
+            adder.tensor_tensor(out=result[:], in0=picked[:, 0, :], in1=picked[:, 1, :], op=ALU.add)
+            queue = nc.scalar if is_last else nc.sync
+            queue.dma_start(out=out[a * P:(a + 1) * P, first * P:(first + count) * P], in_=result[:])

from contextlib import ExitStack

import concourse.mybir as mybir
from concourse.masks import make_identity

F32 = mybir.dt.float32
BF16 = mybir.dt.bfloat16
I32 = mybir.dt.int32
U32 = mybir.dt.uint32
U16 = mybir.dt.uint16
U8 = mybir.dt.uint8
E4M3 = mybir.dt.float8_e4m3fn_x4
E5M2 = mybir.dt.float8_e5m2_x4
E2M1 = mybir.dt.float4_e2m1fn_x4
ACT = mybir.ActivationFunctionType
ALU = mybir.AluOpType

P = 128
PACK = 4
FEAT = 512
NODES = 1024
DEG = 2
PLANES = FEAT // P
BLOCKS = NODES // P
BANK = 512
HALVES = NODES // BANK
HALF_BLOCKS = BANK // P
LIST_ROWS = 16
BLOCK_COLUMNS = P * DEG // LIST_ROWS
ALIGN = 64
DY_CHUNK = 256
VECTOR_CAST = 144
WINDOW = 1376
PICKED_BUFS = 7
GPSIMD_PRODUCTS = 5
GPSIMD_SHIFTS = 4
DH_GROUPS = ((0, 4), (4, 2), (6, 1), (7, 1))
FLOPS = 2 * 2 * FEAT * FEAT * NODES


def tile_attend_ggcn2_tnh_kernel(tc, dyT, w2, w1_words, w1_scales, hT, offs, out):
    nc = tc.nc
    last_plane = PLANES - 1
    with ExitStack() as ctx:
        keep = ctx.enter_context(tc.tile_pool(name="keep", bufs=1))
        ring = ctx.enter_context(tc.tile_pool(name="ring", bufs=2))
        psum = ctx.enter_context(tc.psum_pool(name="psum", bufs=1))

        offsets = keep.tile([P, NODES * DEG // LIST_ROWS], U16, name="offsets")
        ident = keep.tile([P, P], F32, name="ident")
        w1_sc = keep.tile([P, FEAT], U8, name="w1_sc", align_bytes=ALIGN)
        w1_cd = keep.tile([P, 2 * FEAT], U8, name="w1_cd", align_bytes=ALIGN)

        w2_rows = w2.rearrange("(p t) f -> p t f", t=PACK)
        dy_rows = dyT.rearrange("(p t) x -> p t x", t=PACK)
        h_rows = hT.rearrange("(a p) x -> p a x", p=P)

        def load(name, src, width):
            raw = keep.tile([P, src.shape[1], width], F32, name=name)
            nc.sync.dma_start(out=raw[:], in_=src)
            return raw

        w2_first = load("w2_first", w2_rows[:, :, 0:P], P)
        dy_raw = [load(f"dy_raw{x0}", dy_rows[:, :, x0:x0 + DY_CHUNK], DY_CHUNK) for x0 in range(0, NODES, DY_CHUNK)]
        w2_second = load("w2_second", w2_rows[:, :, P:2 * P], P)
        nc.sync.dma_start(offsets[:], offs)
        w2_rest = load("w2_rest", w2_rows[:, :, 2 * P:FEAT], 2 * P)
        h_raw = [load(f"h_raw{c}", h_rows[:, :, c * 2 * P:(c + 1) * 2 * P], 2 * P) for c in range(BLOCKS // 2)]

        u_all = keep.tile([P, last_plane * NODES + WINDOW], F32, name="u_all")
        w_all = keep.tile([P, last_plane * NODES + WINDOW], F32, name="w_all")
        for table in (u_all, w_all):
            nc.vector.memset(table[:, PLANES * NODES:], 0.0)
        starts = [(last_plane - a) * NODES for a in range(PLANES)]
        u_win = [u_all[:, start:start + WINDOW] for start in starts]
        w_win = [w_all[:, start:start + WINDOW] for start in starts]
        make_identity(nc, ident[:])

        nc.gpsimd.memset(w1_sc[:].bitcast(U32), 0)
        nc.sync.dma_start(out=w1_cd[:].bitcast(I32), in_=w1_words[0].bitcast(I32))
        for q in range(4):
            nc.sync.dma_start(out=w1_sc[32 * q:32 * q + 4, :].bitcast(I32),
                              in_=w1_scales[0, 4 * q:4 * q + 4, :].bitcast(I32))

        def interleave(copy, dst, src):
            copy(out=dst.rearrange("p (c i) t -> p c t i", i=4), in_=src.rearrange("p t (c i) -> p c t i", i=4))

        w2_cd = keep.tile([P, FEAT], U32, name="w2_cd", align_bytes=ALIGN)
        w2_sc = keep.tile([P, FEAT], U8, name="w2_sc", align_bytes=ALIGN)
        w2_raw = [w2_first[:], w2_second[:], w2_rest[:, :, 0:P], w2_rest[:, :, P:2 * P]]

        def quantise_w2(a, copy):
            grouped = keep.tile([P, P, PACK], BF16, name=f"w2_bf{a * P}", align_bytes=ALIGN)
            interleave(copy, grouped[:], w2_raw[a])
            cols = slice(a * P, (a + 1) * P)
            nc.vector.quantize_mx(out=w2_cd[:, cols].bitcast(E4M3), scales=w2_sc[:, cols],
                                  in_=grouped[:].rearrange("p c t -> p (c t)"))

        dy_cd = keep.tile([P, NODES], U32, name="dy_cd", align_bytes=ALIGN)
        dy_sc = keep.tile([P, NODES], U8, name="dy_sc", align_bytes=ALIGN)

        def quantise_dy(c):
            grouped = keep.tile([P, DY_CHUNK, PACK], BF16, name=f"dy_bf{c}", align_bytes=ALIGN)
            interleave(nc.scalar.copy, grouped[:, VECTOR_CAST:, :], dy_raw[c][:, :, VECTOR_CAST:])
            interleave(nc.vector.tensor_copy, grouped[:, :VECTOR_CAST, :], dy_raw[c][:, :, :VECTOR_CAST])
            cols = slice(c * DY_CHUNK, (c + 1) * DY_CHUNK)
            nc.vector.quantize_mx(out=dy_cd[:, cols].bitcast(E5M2), scales=dy_sc[:, cols],
                                  in_=grouped[:].rearrange("p c t -> p (c t)"))

        def upper_product(a, half, copy):
            cols = slice(half * BANK, (half + 1) * BANK)
            acc = psum.tile([P, BANK], F32, name="acc", tag="GH"[half])
            nc.tensor.matmul_mx(out=acc[:], lhsT=w2_cd[:, a * P:(a + 1) * P].bitcast(E4M3),
                                lhsT_scale=w2_sc[:, a * P:(a + 1) * P],
                                rhs=dy_cd[:, cols].bitcast(E5M2), rhs_scale=dy_sc[:, cols], start=True, stop=True)
            copy(out=u_win[a][:, cols], in_=acc[:])

        def look_up(window, first, count, reuse=None):
            if reuse is None:
                picked = ring.tile([P, DEG, count * P], F32, name="picked", tag="picked", bufs=PICKED_BUFS)
            else:
                picked = keep.tile([P, DEG, count * P], F32, name="picked", tag=reuse, align_bytes=ALIGN)
            entries = offsets[:, BLOCK_COLUMNS * first:BLOCK_COLUMNS * (first + count)]
            nc.vector.tensor_copy(out=picked[:].bitcast(U32).rearrange("p j x -> p x j"),
                                  in_=window.bitcast(U32).indirect(entries))
            return picked

        h_term = [keep.tile([P, FEAT], F32, name=f"h_term{b}", tag=f"h_term{b}", align_bytes=ALIGN)
                  for b in range(BLOCKS)]

        def make_h_term(b):
            turned = psum.tile([P, PLANES, P], F32, name="turned", tag="ABCDEFGH"[b])
            for a in range(PLANES):
                nc.tensor.transpose(turned[:, a, :], h_raw[b // 2][:, a, (b % 2) * P:(b % 2 + 1) * P], ident[:])
            turned_row = turned[:].rearrange("p a f -> p (a f)")
            if b >= GPSIMD_PRODUCTS:
                nc.scalar.activation(out=h_term[b][:], in_=turned_row, func=ACT.Square)
                return
            squared = keep.tile([P, FEAT], F32, name="squared", tag=f"squared{b}", align_bytes=ALIGN)
            nc.scalar.activation(out=squared[:], in_=turned_row, func=ACT.Square)
            if b < GPSIMD_SHIFTS:
                nc.gpsimd.tensor_scalar(out=h_term[b][:], in0=squared[:], scalar1=1.0, scalar2=-1.0,
                                        op0=ALU.mult, op1=ALU.add)
            else:
                nc.scalar.activation(out=h_term[b][:], in_=squared[:], func=ACT.Copy, scale=1.0, bias=-1.0)

        dh_cd = {}
        dh_sc = [keep.tile([P, BANK], U8, name=f"dh_sc{half}", align_bytes=ALIGN) for half in range(HALVES)]
        dh_bf = [keep.tile([P, count * P * PACK], BF16, name=f"dh_bf{first}", align_bytes=ALIGN)
                 for first, count in DH_GROUPS]
        su = {}
        minus_dh = {}
        su_banks = "ABCDABCE"

        def first_sum(a, first, count, reuse=None):
            picked = look_up(u_win[a], first, count, reuse)
            for k in range(count):
                if a == 0:
                    su[first + k] = psum.tile([P, PLANES, P], F32, name="su", tag=su_banks[first + k])
                for j in range(DEG):
                    nc.tensor.matmul(su[first + k][:, a, :], picked[:, j, k * P:(k + 1) * P], ident[:],
                                     is_transpose=True, start=(j == 0), stop=(j == DEG - 1))

        def through_tanh(b):
            minus_dh[b] = keep.tile([P, FEAT], BF16, name=f"minus_dh{b}")
            sums = su[b][:].rearrange("p a f -> p (a f)")
            if b < GPSIMD_PRODUCTS:
                su_sb = keep.tile([P, FEAT], F32, name="su_sb", tag=f"su_sb{b}", align_bytes=ALIGN)
                nc.scalar.copy(out=su_sb[:], in_=sums)
                nc.gpsimd.tensor_tensor(out=minus_dh[b][:], in0=su_sb[:], in1=h_term[b][:], op=ALU.mult)
            else:
                nc.vector.scalar_tensor_tensor(out=minus_dh[b][:], in0=h_term[b][:], scalar=1.0, in1=sums,
                                               op0=ALU.subtract, op1=ALU.mult)

        def turn_back(first, count, bank):
            back = psum.tile([P, 2, count * P], F32, name="back", tag=bank)
            for k in range(count):
                words = minus_dh[first + k][:].bitcast(F32)
                for s in range(2):
                    nc.tensor.transpose(back[:, s, k * P:(k + 1) * P], words[:, s::2], ident[:])
            g = max(i for i, group in enumerate(DH_GROUPS) if group[0] <= first)
            k0 = first - DH_GROUPS[g][0]
            dst = dh_bf[g][:].bitcast(F32)[:, 2 * P * k0:2 * P * (k0 + count)]
            nc.scalar.copy(out=dst.rearrange("p (x s) -> p x s", s=2), in_=back[:].rearrange("p s x -> p x s"))

        def quantise_dh(g):
            first, count = DH_GROUPS[g]
            half, k = divmod(first, HALF_BLOCKS)
            if k == 0:
                dh_cd[half] = keep.tile([P, BANK], U32, name=f"dh_cd{half}", align_bytes=ALIGN,
                                        tag=f"h_term{BLOCKS - 1}" if half == 0 else "dh_cd1")
            cols = slice(k * P, (k + count) * P)
            nc.vector.quantize_mx(out=dh_cd[half][:, cols].bitcast(E5M2), scales=dh_sc[half][:, cols],
                                  in_=dh_bf[g][:])

        def lower_product(a, half, on_vector):
            cols = slice(half * BANK, (half + 1) * BANK)
            acc = psum.tile([P, BANK], F32, name="acc", tag="GH"[half])
            nc.tensor.matmul_mx(out=acc[:], lhsT=w1_cd[:, 2 * a * P:2 * (a + 1) * P].bitcast(E2M1),
                                lhsT_scale=w1_sc[:, a * P:(a + 1) * P],
                                rhs=dh_cd[half][:].bitcast(E5M2), rhs_scale=dh_sc[half][:], start=True, stop=True)
            if on_vector:
                nc.vector.tensor_scalar_mul(w_win[a][:, cols], acc[:], -1.0)
            else:
                nc.scalar.activation(out=w_win[a][:, cols], in_=acc[:], func=ACT.Copy, scale=-1.0)

        chunks_in_half = BANK // DY_CHUNK
        quantise_w2(0, nc.vector.tensor_copy)
        for half in range(HALVES):
            for c in range(half * chunks_in_half, (half + 1) * chunks_in_half):
                quantise_dy(c)
            upper_product(0, half, nc.vector.tensor_copy if half == HALVES - 1 else nc.scalar.copy)

        for a in range(1, PLANES):
            quantise_w2(a, nc.scalar.copy)
            for half in range(HALVES):
                upper_product(a, half, nc.scalar.copy)
        for b in range(HALF_BLOCKS):
            make_h_term(b)
        for a in range(last_plane):
            first_sum(a, 0, HALF_BLOCKS)
        first_sum(last_plane, 0, 2)
        first_sum(last_plane, 2, 2)
        for b in range(HALF_BLOCKS):
            through_tanh(b)
        for b in range(HALF_BLOCKS, BLOCKS):
            make_h_term(b)
        turn_back(0, 2, "D")

        for a in range(PLANES):
            first_sum(a, 4, 2, f"squared{a}" if a < last_plane else None)
        through_tanh(4)
        through_tanh(5)
        turn_back(2, 2, "B")
        turn_back(4, 2, "D")

        for a in range(last_plane):
            first_sum(a, 6, 2, f"su_sb{a}")
        first_sum(last_plane, 6, 1, f"su_sb{last_plane}")
        first_sum(last_plane, 7, 1, f"h_term{last_plane}")
        through_tanh(6)
        turn_back(6, 1, "F")
        through_tanh(7)
        turn_back(7, 1, "C")

        quantise_dh(0)
        lower_product(0, 0, on_vector=False)
        for g in range(1, len(DH_GROUPS)):
            quantise_dh(g)
        lower_product(0, 1, on_vector=True)
        for a in range(1, PLANES):
            for half in range(HALVES):
                lower_product(a, half, on_vector=False)

        pieces = [(a, first, HALF_BLOCKS) for a in range(last_plane) for first in (0, HALF_BLOCKS)]
        pieces += [(last_plane, 0, 4), (last_plane, 4, 2), (last_plane, 6, 1), (last_plane, 7, 1)]
        for i, (a, first, count) in enumerate(pieces):
            picked = look_up(w_win[a], first, count)
            result = keep.tile([P, count * P], F32, name=f"res{i}")
            is_last = i == len(pieces) - 1
            adder = nc.vector if is_last else nc.gpsimd
            adder.tensor_tensor(out=result[:], in0=picked[:, 0, :], in1=picked[:, 1, :], op=ALU.add)
            queue = nc.scalar if is_last else nc.sync
            queue.dma_start(out=out[a * P:(a + 1) * P, first * P:(first + count) * P], in_=result[:])
